import numpy as np
import ml_dtypes


def mxq(x, axis, fmt="e4m3"):
    dtype, down = {"e4m3": (ml_dtypes.float8_e4m3fn, 7), "e5m2": (ml_dtypes.float8_e5m2, 14)}[fmt]
    v = np.moveaxis(np.asarray(x, np.float32).astype(ml_dtypes.bfloat16).astype(np.float64), axis, -1)
    blocks = v.reshape(v.shape[:-1] + (-1, 32))
    amax = np.abs(blocks).max(-1, keepdims=True)
    byte = np.maximum(np.where(amax > 0, np.frexp(amax)[1] - 1 + 127, 0) - down, 1)
    scale = np.exp2(byte - 127.0)
    codes = (blocks / scale).astype(np.float32).astype(dtype).astype(np.float64)
    return np.moveaxis((codes * scale).reshape(v.shape), -1, axis)


WIDE = False


def mx_kscale(k):
    if not WIDE:
        return np.ones(k)
    levels = np.array([10, -10, 5, -5, 0])
    if k % 512:
        return np.exp2(np.random.permutation(np.resize(levels, k // 32))).repeat(32)
    a = np.empty((k // 512, 16))
    for p in range(k // 512):
        a[p, :8] = np.random.permutation(np.resize(levels, 8))
        for g in range(8):
            far = levels[np.abs(levels - a[p, g]) >= 10]
            a[p, g + 8] = far[np.random.randint(len(far))]
    return np.exp2(a.ravel()).repeat(32)


def f64(x):
    return np.asarray(x).astype(np.float64)


def striped(idx):
    return np.tile(idx.reshape(-1, 16).T, (8, 1)).astype(np.uint16)


def unstriped(offs):
    return offs[:16].T.reshape(-1).astype(np.int64)


E2M1 = np.array([0.0, 0.5, 1.0, 1.5, 2.0, 3.0, 4.0, 6.0, -0.0, -0.5, -1.0, -1.5, -2.0, -3.0, -4.0, -6.0])


def pack_weight(w, fmt):
    k, n = w.shape
    w = f64(np.asarray(w, np.float32).astype(ml_dtypes.bfloat16)).reshape(k // 32, 32, n)
    amax = np.abs(w).max(1)
    if fmt == "e4m3":
        byte = np.frexp(amax)[1] - 1 + 127 - 7
    else:
        mant, ex = np.frexp(amax / 6.0)
        byte = np.where(mant > 0.5, ex, ex - 1) + 127
    byte = np.clip(np.where(amax > 0, byte, 1), 1, 254)
    scaled = (w * np.exp2(127.0 - byte)[:, None, :]).reshape(k, n).astype(np.float32)
    by_word = np.ascontiguousarray(scaled.reshape(k // 512, 128, 4, n).transpose(0, 1, 3, 2))
    if fmt == "e4m3":
        words = by_word.astype(ml_dtypes.float8_e4m3fn).view(np.uint8)
    else:
        c = by_word.astype(ml_dtypes.float4_e2m1fn).view(np.uint8) & 0xF
        words = (c[..., 0::2] | (c[..., 1::2] << 4)).reshape(k // 512, 128, 2 * n)
    return np.ascontiguousarray(words), np.ascontiguousarray(byte.astype(np.uint8).reshape(k // 512, 16, n))


def unpack_weight(words, scales, fmt):
    g, _, n = scales.shape
    words = np.ascontiguousarray(words).reshape(g, 128, n, -1)
    if fmt == "e4m3":
        vals = words.view(ml_dtypes.float8_e4m3fn).astype(np.float64)
    else:
        nib = np.empty((g, 128, n, 4), np.uint8)
        nib[..., 0::2] = words & 0xF
        nib[..., 1::2] = words >> 4
        vals = E2M1[nib]
    vals = vals * np.repeat(np.exp2(scales.astype(np.float64) - 127.0), 8, axis=1)[..., None]
    return vals.transpose(0, 1, 3, 2).reshape(g * 512, n)


def relu(v):
    return np.maximum(v, 0.0)


K, T, G, C1, E, C2, H = 1024, 1024, 2, 512, 8, 128, 512
N = 256


def by_expert(wq, xq, E, C):
    return np.concatenate([wq[e].T @ xq[:, e * C:(e + 1) * C] for e in range(E)], axis=1)


def setup_inputs():
    n = np.random.standard_normal
    s = mx_kscale(K)
    u = mx_kscale(H)
    slots1 = np.random.permutation(T)
    slots2 = np.concatenate([q * C1 + np.random.permutation(C1) for q in range(G)])
    x = pack_weight(n((K, T)) * s[:, None], "e4m3")
    wg = [pack_weight(m, "e2m1") for m in n((G, K, H)) / np.sqrt(K) / s[None, :, None] * u]
    return {
        "x_words": x[0],
        "x_scales": x[1],
        "wg_words": np.stack([m[0] for m in wg]),
        "wg_scales": np.stack([m[1] for m in wg]),
        "we": (n((E, H, N)) / np.sqrt(H) / u[None, :, None]).astype(np.float32),
        "gate": (np.tile(np.random.uniform(0.2, 1.0, T), (128, 1))).astype(np.float32),
        "offs": striped(slots1),
        "offs2": striped(slots2),
        "dst": striped(slots1[slots2]),
    }


def reference(x_words, x_scales, wg_words, wg_scales, we, gate, offs, offs2, dst):
    wg = np.stack([unpack_weight(wg_words[e], wg_scales[e], "e2m1") for e in range(G)])
    weq = mxq(f64(we), 1, "e4m3")
    idx, idx2 = unstriped(offs), unstriped(offs2)
    xq = unpack_weight(x_words, x_scales, "e4m3")[:, idx]
    a = relu(by_expert(wg, xq, G, C1))
    y = by_expert(weq, mxq(a[:, idx2], 0, "e4m3"), E, C2)
    out = np.zeros((N, T))
    out[:, unstriped(dst)] = f64(gate[:1]) * y
    return out

@@ -1,0 +1,272 @@
+from contextlib import ExitStack
+
+import concourse.mybir as mybir
+from concourse.masks import make_identity
+
+K, T, G, C1, E, C2, H, N = 1024, 1024, 2, 512, 8, 128, 512, 256
+FLOPS = 2 * K * H * T + 2 * H * N * T
+
+F32 = mybir.dt.float32
+BF16 = mybir.dt.bfloat16
+I32 = mybir.dt.int32
+U32 = mybir.dt.uint32
+U16 = mybir.dt.uint16
+U8 = mybir.dt.uint8
+FP8X4 = mybir.dt.float8_e4m3fn_x4
+FP4X4 = mybir.dt.float4_e2m1fn_x4
+RELU = mybir.ActivationFunctionType.Relu
+MULT = mybir.AluOpType.mult
+
+P = 128
+PASSES = K // 512
+PIECE = 256
+PIECES = T // PIECE
+LIST_COLS = PIECE // 16
+
+
+def tile_moe_hie_relu_kernel(
+    tc, x_words, x_scales, wg_words, wg_scales, we, gate, offs, offs2, dst, out
+):
+    nc = tc.nc
+    with ExitStack() as ctx:
+        held = ctx.enter_context(tc.tile_pool(name="held", bufs=1))
+        first_psum = ctx.enter_context(tc.psum_pool(name="first_psum", bufs=4))
+        turn_psum = ctx.enter_context(tc.psum_pool(name="turn_psum", bufs=1))
+        second_psum = ctx.enter_context(tc.psum_pool(name="second_psum", bufs=2))
+
+        offs_t = held.tile([P, T // 16], U16, name="offs_t")
+        offs2_t = held.tile([P, T // 16], U16, name="offs2_t")
+        dst_t = held.tile([P, T // 16], U16, name="dst_t")
+        x_w = [held.tile([P, T], I32, name=f"x_w{s}", align_bytes=64) for s in range(PASSES)]
+        x_s = held.tile([P, PASSES * T], U8, name="x_s", align_bytes=64)
+        wg_w = [held.tile([P, PASSES * 2 * H], U8, name=f"wg_w{f}", align_bytes=64) for f in range(G)]
+        wg_s = held.tile([P, G * PASSES * H], U8, name="wg_s", align_bytes=64)
+        we_raw = [held.tile([P, 4 * N], F32, name=f"we_raw{e}") for e in range(E)]
+        gate_t = held.tile([P, T], F32, name="gate_t")
+        ident = held.tile([P, P], F32, name="ident")
+        pairs = [held.tile([P, T], F32, name=f"pairs{u}", align_bytes=64) for u in range(2)]
+        result = [held.tile([P, T], F32, name=f"result{h}") for h in range(N // P)]
+
+        nc.gpsimd.memset(x_s[:].bitcast(I32), 0)
+        nc.vector.memset(wg_s[:].bitcast(I32), 0)
+        make_identity(nc, ident[:])
+
+        def load_we(e):
+            nc.sync.dma_start(out=we_raw[e][:], in_=we[e].rearrange("(p j) n -> p (j n)", j=4))
+
+        def load_wg(f):
+            nc.sync.dma_start(
+                out=wg_w[f][:].bitcast(I32).rearrange("p (s w) -> p s w", s=PASSES),
+                in_=wg_words[f].bitcast(I32).rearrange("s p w -> p s w"),
+            )
+
+        def load_x(s):
+            nc.sync.dma_start(out=x_w[s][:], in_=x_words[s].rearrange("p t d -> p (t d)").bitcast(I32))
+
+        nc.sync.dma_start(offs_t[:], offs)
+        load_x(0)
+        for q in range(4):
+            nc.sync.dma_start(
+                out=x_s[32 * q : 32 * q + 4, :].bitcast(I32).rearrange("b (s w) -> b s w", s=PASSES),
+                in_=x_scales[:, 4 * q : 4 * q + 4, :].bitcast(I32).rearrange("s b w -> b s w"),
+            )
+        load_x(1)
+        load_wg(0)
+        for q in range(4):
+            nc.sync.dma_start(
+                out=wg_s[32 * q : 32 * q + 4, :].bitcast(I32).rearrange("b (a w) -> b a w", a=G * PASSES),
+                in_=wg_scales[:, :, 4 * q : 4 * q + 4, :].bitcast(I32).rearrange("f s b w -> b (f s) w"),
+            )
+        load_we(0)
+        load_we(1)
+        load_wg(1)
+        nc.sync.dma_start(offs2_t[:], offs2)
+        load_we(2)
+        load_we(3)
+        nc.sync.dma_start(dst_t[:], dst)
+        nc.sync.dma_start(out=gate_t[:], in_=gate)
+        for e in range(4, E):
+            load_we(e)
+
+        def entries(list_tile, c):
+            return list_tile[:, c * LIST_COLS : (c + 1) * LIST_COLS]
+
+        tok_w, tok_s, sums, turned, we_bf, we_q, picked, woven, a_q, y_ps, y_sb = {}, {}, {}, {}, {}, {}, {}, {}, {}, {}, {}
+
+        def gather_tokens(c):
+            for s in range(PASSES):
+                w = held.tile([P, PIECE], U32, name=f"tok_w{s}", bufs=2, align_bytes=64)
+                b = held.tile([P, PIECE], U8, name=f"tok_s{s}", bufs=2, align_bytes=64)
+                nc.vector.tensor_copy(b[:], x_s[:, s * T : (s + 1) * T].indirect(entries(offs_t, c)))
+                nc.vector.tensor_copy(w[:], x_w[s][:].bitcast(U32).indirect(entries(offs_t, c)))
+                tok_w[c, s] = w
+                tok_s[c, s] = b
+
+        def first_product(j):
+            c, half, f = j // 2, j % 2, j // 4
+            acc = first_psum.tile([P, H], F32, name="acc")
+            cols = slice(half * P, (half + 1) * P)
+            for s in range(PASSES):
+                a = f * PASSES + s
+                nc.tensor.matmul_mx(
+                    out=acc[:],
+                    lhsT=tok_w[c, s][:, cols].bitcast(FP8X4),
+                    lhsT_scale=tok_s[c, s][:, cols],
+                    rhs=wg_w[f][:, s * 2 * H : (s + 1) * 2 * H].bitcast(FP4X4),
+                    rhs_scale=wg_s[:, a * H : (a + 1) * H],
+                    start=(s == 0),
+                    stop=(s == PASSES - 1),
+                )
+            sums[j] = acc
+
+        def relu_and_turn(j):
+            f, place = j // 4, j % 4
+            a_t = held.tile([P, H], BF16, name=f"a_t{j}", align_bytes=64)
+            nc.scalar.activation(
+                out=a_t[:].rearrange("m (u p v) -> m u p v", u=2, v=2),
+                in_=sums[j][:].rearrange("m (p u v) -> m u p v", u=2, v=2),
+                func=RELU,
+            )
+            for u in range(2):
+                if place == 0:
+                    turned[f, u] = turn_psum.tile([P, C1], F32, name=f"turned{u}")
+                nc.tensor.transpose(
+                    turned[f, u][:, place * P : (place + 1) * P],
+                    a_t[:].bitcast(F32)[:, u * P : (u + 1) * P],
+                    ident[:],
+                )
+
+        def keep_pairs(f):
+            for u in range(2):
+                nc.scalar.copy(out=pairs[u][:, f * C1 : (f + 1) * C1], in_=turned[f, u][:])
+
+        def round_we(e):
+            w = held.tile([P, 4 * N], BF16, name=f"we_bf{e}", align_bytes=64)
+            nc.scalar.copy(
+                out=w[:].rearrange("p (c i j) -> p c j i", i=4, j=4),
+                in_=we_raw[e][:].rearrange("p (j c i) -> p c j i", i=4, j=4),
+            )
+            we_bf[e] = w
+
+        def quantise_we(e):
+            codes = held.tile([P, N], U32, name=f"we_codes{e}", align_bytes=64)
+            scales = held.tile([P, N], U8, name=f"we_scales{e}", align_bytes=64)
+            nc.vector.quantize_mx(out=codes[:].bitcast(FP8X4), scales=scales[:], in_=we_bf[e][:])
+            we_q[e] = (codes, scales)
+
+        def gather_pairs(c):
+            f = c // 2
+            g = held.tile([P, 2 * PIECE], U32, name=f"picked{c}", align_bytes=64)
+            for u in range(2):
+                window = pairs[u][:, : (f + 1) * C1].bitcast(U32)
+                nc.vector.tensor_copy(g[:, u * PIECE : (u + 1) * PIECE], window.indirect(entries(offs2_t, c)))
+            picked[c] = g
+
+        def weave(c):
+            w = held.tile([P, 2 * PIECE], U32, name=f"woven{c}", align_bytes=64)
+            nc.scalar.copy(
+                out=w[:].rearrange("p (m u) -> p m u", u=2),
+                in_=picked[c][:].rearrange("p (u m) -> p m u", u=2),
+            )
+            woven[c] = w
+
+        def quantise_a(c):
+            codes = held.tile([P, PIECE], U32, name=f"a_codes{c}", align_bytes=64)
+            scales = held.tile([P, PIECE], U8, name=f"a_scales{c}", align_bytes=64)
+            nc.vector.quantize_mx(out=codes[:].bitcast(FP8X4), scales=scales[:], in_=woven[c][:].bitcast(BF16))
+            a_q[c] = (codes, scales)
+
+        def second_product(c):
+            acc = second_psum.tile([P, 2 * PIECE], F32, name="y_acc")
+            for h in range(N // P):
+                for half in range(2):
+                    w_codes, w_scales = we_q[2 * c + half]
+                    a_codes, a_scales = a_q[c]
+                    rows = slice(h * P, (h + 1) * P)
+                    cols = slice(half * C2, (half + 1) * C2)
+                    at = h * PIECE + half * C2
+                    nc.tensor.matmul_mx(
+                        out=acc[:, at : at + C2],
+                        lhsT=w_codes[:, rows].bitcast(FP8X4),
+                        lhsT_scale=w_scales[:, rows],
+                        rhs=a_codes[:, cols].bitcast(FP8X4),
+                        rhs_scale=a_scales[:, cols],
+                        start=True,
+                        stop=True,
+                    )
+            y_ps[c] = acc
+
+        def keep_y(c, h):
+            y = held.tile([P, PIECE], F32, name=f"y{c}_{h}")
+            nc.scalar.copy(out=y[:], in_=y_ps[c][:, h * PIECE : (h + 1) * PIECE])
+            y_sb[c, h] = y
+
+        def scatter(c, h):
+            nc.vector.tensor_tensor(
+                result[h][:].indirect(entries(dst_t, c)),
+                y_sb[c, h][:],
+                gate_t[:, c * PIECE : (c + 1) * PIECE],
+                MULT,
+            )
+
+        def first_level(c):
+            gather_tokens(c)
+            first_product(2 * c)
+            first_product(2 * c + 1)
+
+        def put_back(c, h):
+            keep_y(c, h)
+            scatter(c, h)
+
+        def round_and_quantise_we(e):
+            round_we(e)
+            quantise_we(e)
+
+        def weave_and_quantise(c):
+            weave(c)
+            quantise_a(c)
+
+        first_level(0)
+        first_level(1)
+        relu_and_turn(0)
+        relu_and_turn(1)
+        round_and_quantise_we(0)
+        relu_and_turn(2)
+        relu_and_turn(3)
+        round_and_quantise_we(1)
+        keep_pairs(0)
+        first_level(2)
+        first_level(3)
+        gather_pairs(0)
+        gather_pairs(1)
+        relu_and_turn(4)
+        relu_and_turn(5)
+        weave_and_quantise(0)
+        second_product(0)
+        relu_and_turn(6)
+        relu_and_turn(7)
+        put_back(0, 0)
+        weave_and_quantise(1)
+        round_and_quantise_we(2)
+        put_back(0, 1)
+        round_and_quantise_we(3)
+        second_product(1)
+        keep_pairs(1)
+        gather_pairs(2)
+        gather_pairs(3)
+        put_back(1, 0)
+        round_and_quantise_we(4)
+        weave_and_quantise(2)
+        round_and_quantise_we(5)
+        second_product(2)
+        put_back(1, 1)
+        weave_and_quantise(3)
+        round_and_quantise_we(6)
+        put_back(2, 0)
+        round_and_quantise_we(7)
+        second_product(3)
+        put_back(2, 1)
+        put_back(3, 0)
+        put_back(3, 1)
+        for h in range(2):
+            nc.sync.dma_start(out=out[h * P : (h + 1) * P, :], in_=result[h][:])

@@ -15,7 +15,9 @@ U8 = mybir.dt.uint8
 FP8X4 = mybir.dt.float8_e4m3fn_x4
 FP4X4 = mybir.dt.float4_e2m1fn_x4
 RELU = mybir.ActivationFunctionType.Relu
+COPY = mybir.ActivationFunctionType.Copy
 MULT = mybir.AluOpType.mult
+ADD = mybir.AluOpType.add
 
 P = 128
 PASSES = K // 512
@@ -30,9 +32,9 @@ def tile_moe_hie_relu_kernel(
     nc = tc.nc
     with ExitStack() as ctx:
         held = ctx.enter_context(tc.tile_pool(name="held", bufs=1))
-        first_psum = ctx.enter_context(tc.psum_pool(name="first_psum", bufs=4))
+        first_psum = ctx.enter_context(tc.psum_pool(name="first_psum", bufs=3))
         turn_psum = ctx.enter_context(tc.psum_pool(name="turn_psum", bufs=1))
-        second_psum = ctx.enter_context(tc.psum_pool(name="second_psum", bufs=2))
+        second_psum = ctx.enter_context(tc.psum_pool(name="second_psum", bufs=3))
 
         offs_t = held.tile([P, T // 16], U16, name="offs_t")
         offs2_t = held.tile([P, T // 16], U16, name="offs2_t")
@@ -42,14 +44,16 @@ def tile_moe_hie_relu_kernel(
         wg_w = [held.tile([P, PASSES * 2 * H], U8, name=f"wg_w{f}", align_bytes=64) for f in range(G)]
         wg_s = held.tile([P, G * PASSES * H], U8, name="wg_s", align_bytes=64)
         we_raw = [held.tile([P, 4 * N], F32, name=f"we_raw{e}") for e in range(E)]
-        gate_t = held.tile([P, T], F32, name="gate_t")
         ident = held.tile([P, P], F32, name="ident")
-        pairs = [held.tile([P, T], F32, name=f"pairs{u}", align_bytes=64) for u in range(2)]
+        ident_bf = held.tile([P, P], BF16, name="ident_bf")
+        a_kept = held.tile([P, G * 4 * C1], BF16, name="a_kept", align_bytes=64)
+        gate_t = [held.tile([P, C1], F32, name=f"gate_t{f}") for f in range(G)]
         result = [held.tile([P, T], F32, name=f"result{h}") for h in range(N // P)]
 
         nc.gpsimd.memset(x_s[:].bitcast(I32), 0)
         nc.vector.memset(wg_s[:].bitcast(I32), 0)
         make_identity(nc, ident[:])
+        make_identity(nc, ident_bf[:])
 
         def load_we(e):
             nc.sync.dma_start(out=we_raw[e][:], in_=we[e].rearrange("(p j) n -> p (j n)", j=4))
@@ -79,14 +83,15 @@ def tile_moe_hie_relu_kernel(
             )
         load_we(0)
         load_we(1)
-        load_wg(1)
         nc.sync.dma_start(offs2_t[:], offs2)
         load_we(2)
-        load_we(3)
-        nc.sync.dma_start(dst_t[:], dst)
-        nc.sync.dma_start(out=gate_t[:], in_=gate)
-        for e in range(4, E):
+        load_wg(1)
+        for e in range(3, 7):
             load_we(e)
+        nc.sync.dma_start(dst_t[:], dst)
+        nc.sync.dma_start(out=gate_t[0][:], in_=gate[:, :C1])
+        load_we(7)
+        nc.sync.dma_start(out=gate_t[1][:], in_=gate[:, C1:])
 
         def entries(list_tile, c):
             return list_tile[:, c * LIST_COLS : (c + 1) * LIST_COLS]
@@ -95,70 +100,104 @@ def tile_moe_hie_relu_kernel(
 
         def gather_tokens(c):
             for s in range(PASSES):
-                w = held.tile([P, PIECE], U32, name=f"tok_w{s}", bufs=2, align_bytes=64)
-                b = held.tile([P, PIECE], U8, name=f"tok_s{s}", bufs=2, align_bytes=64)
+                w = held.tile([P, PIECE], U32, name=f"tok_w{c}_{s}", tag=f"words{c % 2}_{s}", align_bytes=64)
+                b = held.tile([P, PIECE], U8, name=f"tok_s{c}_{s}", tag=f"bytes{c % 2}_{s}", align_bytes=64)
                 nc.vector.tensor_copy(b[:], x_s[:, s * T : (s + 1) * T].indirect(entries(offs_t, c)))
                 nc.vector.tensor_copy(w[:], x_w[s][:].bitcast(U32).indirect(entries(offs_t, c)))
                 tok_w[c, s] = w
                 tok_s[c, s] = b
 
-        def first_product(j):
-            c, half, f = j // 2, j % 2, j // 4
-            acc = first_psum.tile([P, H], F32, name="acc")
-            cols = slice(half * P, (half + 1) * P)
+        def first_products(c):
+            f = c // 2
+            for half in range(2):
+                sums[2 * c + half] = first_psum.tile([P, H], F32, name="acc")
             for s in range(PASSES):
                 a = f * PASSES + s
-                nc.tensor.matmul_mx(
-                    out=acc[:],
-                    lhsT=tok_w[c, s][:, cols].bitcast(FP8X4),
-                    lhsT_scale=tok_s[c, s][:, cols],
-                    rhs=wg_w[f][:, s * 2 * H : (s + 1) * 2 * H].bitcast(FP4X4),
-                    rhs_scale=wg_s[:, a * H : (a + 1) * H],
-                    start=(s == 0),
-                    stop=(s == PASSES - 1),
-                )
-            sums[j] = acc
+                for half in range(2):
+                    cols = slice(half * P, (half + 1) * P)
+                    nc.tensor.matmul_mx(
+                        out=sums[2 * c + half][:],
+                        lhsT=tok_w[c, s][:, cols].bitcast(FP8X4),
+                        lhsT_scale=tok_s[c, s][:, cols],
+                        rhs=wg_w[f][:, s * 2 * H : (s + 1) * 2 * H].bitcast(FP4X4),
+                        rhs_scale=wg_s[:, a * H : (a + 1) * H],
+                        start=(s == 0),
+                        stop=(s == PASSES - 1),
+                    )
 
-        def relu_and_turn(j):
-            f, place = j // 4, j % 4
+        def relu_and_turn_pairs(j):
+            c, half = j // 2, j % 2
             a_t = held.tile([P, H], BF16, name=f"a_t{j}", align_bytes=64)
             nc.scalar.activation(
                 out=a_t[:].rearrange("m (u p v) -> m u p v", u=2, v=2),
                 in_=sums[j][:].rearrange("m (p u v) -> m u p v", u=2, v=2),
                 func=RELU,
             )
+            if half == 0:
+                turned[c] = turn_psum.tile([P, 2 * PIECE], F32, name=f"turned{c % 2}")
             for u in range(2):
-                if place == 0:
-                    turned[f, u] = turn_psum.tile([P, C1], F32, name=f"turned{u}")
-                nc.tensor.transpose(
-                    turned[f, u][:, place * P : (place + 1) * P],
-                    a_t[:].bitcast(F32)[:, u * P : (u + 1) * P],
-                    ident[:],
+                at = u * PIECE + half * P
+                nc.tensor.transpose(turned[c][:, at : at + P], a_t[:].bitcast(F32)[:, u * P : (u + 1) * P], ident[:])
+
+        def relu_and_turn_planes(j):
+            c, half = j // 2, j % 2
+            a_t = held.tile([P, H], BF16, name=f"a_t{j}", align_bytes=64)
+            nc.scalar.activation(
+                out=a_t[:].rearrange("m (t p) -> m t p", t=4),
+                in_=sums[j][:].rearrange("m (p t) -> m t p", t=4),
+                func=RELU,
+            )
+            if half == 0:
+                turned[c] = turn_psum.tile([P, 4 * PIECE], BF16, name=f"turned{c % 2}")
+            for t in range(4):
+                at = t * PIECE + half * P
+                nc.tensor.transpose(turned[c][:, at : at + P], a_t[:, t * P : (t + 1) * P], ident_bf[:])
+
+        def keep_pairs(c):
+            by_pair = a_kept[:].bitcast(F32)[:, : 2 * C1].rearrange("p (u m) -> p u m", u=2)
+            nc.scalar.copy(
+                out=by_pair[:, :, c * PIECE : (c + 1) * PIECE],
+                in_=turned[c][:].rearrange("p (u m) -> p u m", u=2),
+            )
+
+        def keep_planes(c):
+            by_plane = a_kept[:, 4 * C1 :].rearrange("p (t m) -> p t m", t=4)
+            nc.scalar.copy(
+                out=by_plane[:, :, (c - 2) * PIECE : (c - 1) * PIECE],
+                in_=turned[c][:].rearrange("p (t m) -> p t m", t=4),
+            )
+
+        def round_we(e, engine):
+            if e % 2 == 0:
+                we_bf[e // 2] = held.tile([P, 2 * 4 * N], BF16, name=f"we_bf{e // 2}", align_bytes=64)
+            w = we_bf[e // 2][:, (e % 2) * 4 * N : (e % 2 + 1) * 4 * N]
+            if engine == "gpsimd":
+                nc.gpsimd.tensor_scalar(
+                    w.rearrange("p (n j) -> p n j", j=4),
+                    we_raw[e][:].rearrange("p (j n) -> p n j", j=4),
+                    1.0,
+                    0.0,
+                    MULT,
+                    ADD,
+                )
+            else:
+                copy = nc.scalar.copy if engine == "scalar" else nc.vector.tensor_copy
+                copy(
+                    out=w.rearrange("p (c i j) -> p c j i", i=4, j=4),
+                    in_=we_raw[e][:].rearrange("p (j c i) -> p c j i", i=4, j=4),
                 )
 
-        def keep_pairs(f):
-            for u in range(2):
-                nc.scalar.copy(out=pairs[u][:, f * C1 : (f + 1) * C1], in_=turned[f, u][:])
-
-        def round_we(e):
-            w = held.tile([P, 4 * N], BF16, name=f"we_bf{e}", align_bytes=64)
-            nc.scalar.copy(
-                out=w[:].rearrange("p (c i j) -> p c j i", i=4, j=4),
-                in_=we_raw[e][:].rearrange("p (j c i) -> p c j i", i=4, j=4),
-            )
-            we_bf[e] = w
-
-        def quantise_we(e):
-            codes = held.tile([P, N], U32, name=f"we_codes{e}", align_bytes=64)
-            scales = held.tile([P, N], U8, name=f"we_scales{e}", align_bytes=64)
-            nc.vector.quantize_mx(out=codes[:].bitcast(FP8X4), scales=scales[:], in_=we_bf[e][:])
-            we_q[e] = (codes, scales)
+        def quantise_we(c):
+            tag = f"words1_{1 - c}" if c < 2 else f"we_codes{c}"
+            codes = held.tile([P, 2 * N], U32, name=f"we_codes{c}", tag=tag, align_bytes=64)
+            scales = held.tile([P, 2 * N], U8, name=f"we_scales{c}", align_bytes=64)
+            nc.vector.quantize_mx(out=codes[:].bitcast(FP8X4), scales=scales[:], in_=we_bf[c][:])
+            we_q[c] = (codes, scales)
 
         def gather_pairs(c):
-            f = c // 2
             g = held.tile([P, 2 * PIECE], U32, name=f"picked{c}", align_bytes=64)
             for u in range(2):
-                window = pairs[u][:, : (f + 1) * C1].bitcast(U32)
+                window = a_kept[:].bitcast(U32)[:, u * C1 : (u + 1) * C1]
                 nc.vector.tensor_copy(g[:, u * PIECE : (u + 1) * PIECE], window.indirect(entries(offs2_t, c)))
             picked[c] = g
 
@@ -168,6 +207,14 @@ def tile_moe_hie_relu_kernel(
                 out=w[:].rearrange("p (m u) -> p m u", u=2),
                 in_=picked[c][:].rearrange("p (u m) -> p m u", u=2),
             )
+            woven[c] = w
+
+        def gather_planes(c):
+            w = held.tile([P, 2 * PIECE], U32, name=f"woven{c}", tag="woven_planes", align_bytes=64)
+            by_plane = w[:].bitcast(BF16).rearrange("p (m t) -> p m t", t=4)
+            for t in range(4):
+                window = a_kept[:, (3 + t) * C1 : (5 + t) * C1]
+                nc.scalar.activation(by_plane[:, :, t], window.indirect(entries(offs2_t, c)), COPY)
             woven[c] = w
 
         def quantise_a(c):
@@ -180,9 +227,9 @@ def tile_moe_hie_relu_kernel(
             acc = second_psum.tile([P, 2 * PIECE], F32, name="y_acc")
             for h in range(N // P):
                 for half in range(2):
-                    w_codes, w_scales = we_q[2 * c + half]
+                    w_codes, w_scales = we_q[c]
                     a_codes, a_scales = a_q[c]
-                    rows = slice(h * P, (h + 1) * P)
+                    rows = slice(half * N + h * P, half * N + (h + 1) * P)
                     cols = slice(half * C2, (half + 1) * C2)
                     at = h * PIECE + half * C2
                     nc.tensor.matmul_mx(
@@ -205,66 +252,60 @@ def tile_moe_hie_relu_kernel(
             nc.vector.tensor_tensor(
                 result[h][:].indirect(entries(dst_t, c)),
                 y_sb[c, h][:],
-                gate_t[:, c * PIECE : (c + 1) * PIECE],
+                gate_t[c // 2][:, (c % 2) * PIECE : (c % 2 + 1) * PIECE],
                 MULT,
             )
 
         def first_level(c):
             gather_tokens(c)
-            first_product(2 * c)
-            first_product(2 * c + 1)
+            first_products(c)
 
         def put_back(c, h):
             keep_y(c, h)
             scatter(c, h)
 
-        def round_and_quantise_we(e):
-            round_we(e)
-            quantise_we(e)
-
-        def weave_and_quantise(c):
-            weave(c)
+        def second_level(c):
             quantise_a(c)
+            second_product(c)
 
         first_level(0)
         first_level(1)
-        relu_and_turn(0)
-        relu_and_turn(1)
-        round_and_quantise_we(0)
-        relu_and_turn(2)
-        relu_and_turn(3)
-        round_and_quantise_we(1)
-        keep_pairs(0)
+        round_we(0, "scalar")
+        for c in range(2):
+            relu_and_turn_pairs(2 * c)
+            relu_and_turn_pairs(2 * c + 1)
+            keep_pairs(c)
+        round_we(1, "scalar")
         first_level(2)
         first_level(3)
+        for e in range(2, 7):
+            round_we(e, "gpsimd")
         gather_pairs(0)
         gather_pairs(1)
-        relu_and_turn(4)
-        relu_and_turn(5)
-        weave_and_quantise(0)
-        second_product(0)
-        relu_and_turn(6)
-        relu_and_turn(7)
+        relu_and_turn_planes(4)
+        relu_and_turn_planes(5)
+        keep_planes(2)
+        weave(0)
+        quantise_we(0)
+        second_level(0)
+        relu_and_turn_planes(6)
+        relu_and_turn_planes(7)
+        weave(1)
+        quantise_we(1)
+        second_level(1)
+        quantise_we(2)
         put_back(0, 0)
-        weave_and_quantise(1)
-        round_and_quantise_we(2)
+        keep_planes(3)
         put_back(0, 1)
-        round_and_quantise_we(3)
-        second_product(1)
-        keep_pairs(1)
-        gather_pairs(2)
-        gather_pairs(3)
+        gather_planes(2)
+        second_level(2)
         put_back(1, 0)
-        round_and_quantise_we(4)
-        weave_and_quantise(2)
-        round_and_quantise_we(5)
-        second_product(2)
         put_back(1, 1)
-        weave_and_quantise(3)
-        round_and_quantise_we(6)
+        round_we(7, "vector")
+        quantise_we(3)
         put_back(2, 0)
-        round_and_quantise_we(7)
-        second_product(3)
+        gather_planes(3)
+        second_level(3)
         put_back(2, 1)
         put_back(3, 0)
         put_back(3, 1)

@@ -46,12 +46,14 @@ def tile_moe_hie_relu_kernel(
         we_raw = [held.tile([P, 4 * N], F32, name=f"we_raw{e}") for e in range(E)]
         ident = held.tile([P, P], F32, name="ident")
         ident_bf = held.tile([P, P], BF16, name="ident_bf")
-        a_kept = held.tile([P, G * 4 * C1], BF16, name="a_kept", align_bytes=64)
+        a_pairs = held.tile([P, 3 * C1], F32, name="a_pairs", align_bytes=64)
+        a_planes = [held.tile([P, C1], BF16, name=f"a_plane{t}", align_bytes=64) for t in range(4)]
         gate_t = [held.tile([P, C1], F32, name=f"gate_t{f}") for f in range(G)]
         result = [held.tile([P, T], F32, name=f"result{h}") for h in range(N // P)]
 
         nc.gpsimd.memset(x_s[:].bitcast(I32), 0)
         nc.vector.memset(wg_s[:].bitcast(I32), 0)
+        nc.vector.memset(a_pairs[:, :C1], 0.0)
         make_identity(nc, ident[:])
         make_identity(nc, ident_bf[:])
 
@@ -75,23 +77,22 @@ def tile_moe_hie_relu_kernel(
                 in_=x_scales[:, 4 * q : 4 * q + 4, :].bitcast(I32).rearrange("s b w -> b s w"),
             )
         load_x(1)
-        load_wg(0)
+        load_we(4)
+        load_we(5)
+        load_wg(1)
         for q in range(4):
             nc.sync.dma_start(
                 out=wg_s[32 * q : 32 * q + 4, :].bitcast(I32).rearrange("b (a w) -> b a w", a=G * PASSES),
                 in_=wg_scales[:, :, 4 * q : 4 * q + 4, :].bitcast(I32).rearrange("f s b w -> b (f s) w"),
             )
-        load_we(0)
-        load_we(1)
         nc.sync.dma_start(offs2_t[:], offs2)
-        load_we(2)
-        load_wg(1)
-        for e in range(3, 7):
+        load_we(6)
+        load_wg(0)
+        for e in (7, 0, 1, 2, 3):
             load_we(e)
         nc.sync.dma_start(dst_t[:], dst)
-        nc.sync.dma_start(out=gate_t[0][:], in_=gate[:, :C1])
-        load_we(7)
         nc.sync.dma_start(out=gate_t[1][:], in_=gate[:, C1:])
+        nc.sync.dma_start(out=gate_t[0][:], in_=gate[:, :C1])
 
         def entries(list_tile, c):
             return list_tile[:, c * LIST_COLS : (c + 1) * LIST_COLS]
@@ -140,32 +141,28 @@ def tile_moe_hie_relu_kernel(
                 nc.tensor.transpose(turned[c][:, at : at + P], a_t[:].bitcast(F32)[:, u * P : (u + 1) * P], ident[:])
 
         def relu_and_turn_planes(j):
-            c, half = j // 2, j % 2
             a_t = held.tile([P, H], BF16, name=f"a_t{j}", align_bytes=64)
             nc.scalar.activation(
                 out=a_t[:].rearrange("m (t p) -> m t p", t=4),
                 in_=sums[j][:].rearrange("m (p t) -> m t p", t=4),
                 func=RELU,
             )
-            if half == 0:
-                turned[c] = turn_psum.tile([P, 4 * PIECE], BF16, name=f"turned{c % 2}")
             for t in range(4):
-                at = t * PIECE + half * P
-                nc.tensor.transpose(turned[c][:, at : at + P], a_t[:, t * P : (t + 1) * P], ident_bf[:])
+                if j == 0 and t % 2 == 0:
+                    turned[t // 2] = turn_psum.tile([P, 2 * C1], BF16, name=f"turned{t // 2}")
+                at = (t % 2) * C1 + j * P
+                nc.tensor.transpose(turned[t // 2][:, at : at + P], a_t[:, t * P : (t + 1) * P], ident_bf[:])
 
         def keep_pairs(c):
-            by_pair = a_kept[:].bitcast(F32)[:, : 2 * C1].rearrange("p (u m) -> p u m", u=2)
+            by_pair = a_pairs[:, C1:].rearrange("p (u m) -> p u m", u=2)
             nc.scalar.copy(
-                out=by_pair[:, :, c * PIECE : (c + 1) * PIECE],
+                out=by_pair[:, :, (c - 2) * PIECE : (c - 1) * PIECE],
                 in_=turned[c][:].rearrange("p (u m) -> p u m", u=2),
             )
 
-        def keep_planes(c):
-            by_plane = a_kept[:, 4 * C1 :].rearrange("p (t m) -> p t m", t=4)
-            nc.scalar.copy(
-                out=by_plane[:, :, (c - 2) * PIECE : (c - 1) * PIECE],
-                in_=turned[c][:].rearrange("p (t m) -> p t m", t=4),
-            )
+        def keep_planes():
+            for t in range(4):
+                nc.scalar.copy(out=a_planes[t][:], in_=turned[t // 2][:, (t % 2) * C1 : (t % 2 + 1) * C1])
 
         def round_we(e, engine):
             if e % 2 == 0:
@@ -188,7 +185,7 @@ def tile_moe_hie_relu_kernel(
                 )
 
         def quantise_we(c):
-            tag = f"words1_{1 - c}" if c < 2 else f"we_codes{c}"
+            tag = {2: "words1_1", 3: "woven2", 0: "woven3", 1: "we_codes1"}[c]
             codes = held.tile([P, 2 * N], U32, name=f"we_codes{c}", tag=tag, align_bytes=64)
             scales = held.tile([P, 2 * N], U8, name=f"we_scales{c}", align_bytes=64)
             nc.vector.quantize_mx(out=codes[:].bitcast(FP8X4), scales=scales[:], in_=we_bf[c][:])
@@ -197,12 +194,12 @@ def tile_moe_hie_relu_kernel(
         def gather_pairs(c):
             g = held.tile([P, 2 * PIECE], U32, name=f"picked{c}", align_bytes=64)
             for u in range(2):
-                window = a_kept[:].bitcast(U32)[:, u * C1 : (u + 1) * C1]
+                window = a_pairs[:].bitcast(U32)[:, u * C1 : (u + 2) * C1]
                 nc.vector.tensor_copy(g[:, u * PIECE : (u + 1) * PIECE], window.indirect(entries(offs2_t, c)))
             picked[c] = g
 
         def weave(c):
-            w = held.tile([P, 2 * PIECE], U32, name=f"woven{c}", align_bytes=64)
+            w = held.tile([P, 2 * PIECE], U32, name=f"woven{c}", tag=f"woven{c}", align_bytes=64)
             nc.scalar.copy(
                 out=w[:].rearrange("p (m u) -> p m u", u=2),
                 in_=picked[c][:].rearrange("p (u m) -> p m u", u=2),
@@ -210,11 +207,17 @@ def tile_moe_hie_relu_kernel(
             woven[c] = w
 
         def gather_planes(c):
-            w = held.tile([P, 2 * PIECE], U32, name=f"woven{c}", tag="woven_planes", align_bytes=64)
-            by_plane = w[:].bitcast(BF16).rearrange("p (m t) -> p m t", t=4)
+            g = held.tile([P, 4 * PIECE], BF16, name=f"picked{c}", tag="picked_planes", align_bytes=64)
             for t in range(4):
-                window = a_kept[:, (3 + t) * C1 : (5 + t) * C1]
-                nc.scalar.activation(by_plane[:, :, t], window.indirect(entries(offs2_t, c)), COPY)
+                nc.scalar.activation(g[:, t * PIECE : (t + 1) * PIECE], a_planes[t][:].indirect(entries(offs2_t, c)), COPY)
+            picked[c] = g
+
+        def weave_planes(c):
+            w = held.tile([P, 2 * PIECE], U32, name=f"woven{c}", align_bytes=64)
+            nc.scalar.copy(
+                out=w[:].bitcast(BF16).rearrange("p (m i t) -> p m t i", i=4, t=4),
+                in_=picked[c][:].rearrange("p (t m i) -> p m t i", i=4, t=4),
+            )
             woven[c] = w
 
         def quantise_a(c):
@@ -268,46 +271,46 @@ def tile_moe_hie_relu_kernel(
             quantise_a(c)
             second_product(c)
 
-        first_level(0)
-        first_level(1)
-        round_we(0, "scalar")
-        for c in range(2):
+        first_level(2)
+        first_level(3)
+        round_we(4, "scalar")
+        round_we(5, "scalar")
+        for c in (2, 3):
             relu_and_turn_pairs(2 * c)
             relu_and_turn_pairs(2 * c + 1)
             keep_pairs(c)
-        round_we(1, "scalar")
-        first_level(2)
-        first_level(3)
-        for e in range(2, 7):
+        first_level(0)
+        first_level(1)
+        for e in (6, 7, 0, 1, 2):
             round_we(e, "gpsimd")
-        gather_pairs(0)
-        gather_pairs(1)
-        relu_and_turn_planes(4)
-        relu_and_turn_planes(5)
-        keep_planes(2)
-        weave(0)
-        quantise_we(0)
-        second_level(0)
-        relu_and_turn_planes(6)
-        relu_and_turn_planes(7)
-        weave(1)
-        quantise_we(1)
-        second_level(1)
+        gather_pairs(2)
+        gather_pairs(3)
+        for j in range(4):
+            relu_and_turn_planes(j)
+        weave(2)
         quantise_we(2)
-        put_back(0, 0)
-        keep_planes(3)
-        put_back(0, 1)
-        gather_planes(2)
         second_level(2)
+        keep_planes()
+        weave(3)
+        quantise_we(3)
+        second_level(3)
+        quantise_we(0)
+        put_back(2, 0)
+        put_back(2, 1)
+        gather_planes(0)
+        put_back(3, 0)
+        weave_planes(0)
+        second_level(0)
+        put_back(3, 1)
+        gather_planes(1)
+        put_back(0, 0)
+        weave_planes(1)
+        quantise_a(1)
+        round_we(3, "scalar")
+        quantise_we(1)
+        put_back(0, 1)
+        second_product(1)
         put_back(1, 0)
         put_back(1, 1)
-        round_we(7, "vector")
-        quantise_we(3)
-        put_back(2, 0)
-        gather_planes(3)
-        second_level(3)
-        put_back(2, 1)
-        put_back(3, 0)
-        put_back(3, 1)
         for h in range(2):
             nc.sync.dma_start(out=out[h * P : (h + 1) * P, :], in_=result[h][:])

@@ -281,7 +281,7 @@ def tile_moe_hie_relu_kernel(
             keep_pairs(c)
         first_level(0)
         first_level(1)
-        for e in (6, 7, 0, 1, 2):
+        for e in (6, 7, 0, 1):
             round_we(e, "gpsimd")
         gather_pairs(2)
         gather_pairs(3)
@@ -295,6 +295,7 @@ def tile_moe_hie_relu_kernel(
         quantise_we(3)
         second_level(3)
         quantise_we(0)
+        round_we(2, "vector")
         put_back(2, 0)
         put_back(2, 1)
         gather_planes(0)

from contextlib import ExitStack

import concourse.mybir as mybir
from concourse.masks import make_identity

K, T, G, C1, E, C2, H, N = 1024, 1024, 2, 512, 8, 128, 512, 256
FLOPS = 2 * K * H * T + 2 * H * N * T

F32 = mybir.dt.float32
BF16 = mybir.dt.bfloat16
I32 = mybir.dt.int32
U32 = mybir.dt.uint32
U16 = mybir.dt.uint16
U8 = mybir.dt.uint8
FP8X4 = mybir.dt.float8_e4m3fn_x4
FP4X4 = mybir.dt.float4_e2m1fn_x4
RELU = mybir.ActivationFunctionType.Relu
COPY = mybir.ActivationFunctionType.Copy
MULT = mybir.AluOpType.mult
ADD = mybir.AluOpType.add

P = 128
PASSES = K // 512
PIECE = 256
PIECES = T // PIECE
LIST_COLS = PIECE // 16


def tile_moe_hie_relu_kernel(
    tc, x_words, x_scales, wg_words, wg_scales, we, gate, offs, offs2, dst, out
):
    nc = tc.nc
    with ExitStack() as ctx:
        held = ctx.enter_context(tc.tile_pool(name="held", bufs=1))
        first_psum = ctx.enter_context(tc.psum_pool(name="first_psum", bufs=3))
        turn_psum = ctx.enter_context(tc.psum_pool(name="turn_psum", bufs=1))
        second_psum = ctx.enter_context(tc.psum_pool(name="second_psum", bufs=3))

        offs_t = held.tile([P, T // 16], U16, name="offs_t")
        offs2_t = held.tile([P, T // 16], U16, name="offs2_t")
        dst_t = held.tile([P, T // 16], U16, name="dst_t")
        x_w = [held.tile([P, T], I32, name=f"x_w{s}", align_bytes=64) for s in range(PASSES)]
        x_s = held.tile([P, PASSES * T], U8, name="x_s", align_bytes=64)
        wg_w = [held.tile([P, PASSES * 2 * H], U8, name=f"wg_w{f}", align_bytes=64) for f in range(G)]
        wg_s = held.tile([P, G * PASSES * H], U8, name="wg_s", align_bytes=64)
        we_raw = [held.tile([P, 4 * N], F32, name=f"we_raw{e}") for e in range(E)]
        ident = held.tile([P, P], F32, name="ident")
        ident_bf = held.tile([P, P], BF16, name="ident_bf")
        a_pairs = held.tile([P, 3 * C1], F32, name="a_pairs", align_bytes=64)
        a_planes = [held.tile([P, C1], BF16, name=f"a_plane{t}", align_bytes=64) for t in range(4)]
        gate_t = [held.tile([P, C1], F32, name=f"gate_t{f}") for f in range(G)]
        result = [held.tile([P, T], F32, name=f"result{h}") for h in range(N // P)]

        nc.gpsimd.memset(x_s[:].bitcast(I32), 0)
        nc.vector.memset(wg_s[:].bitcast(I32), 0)
        nc.vector.memset(a_pairs[:, :C1], 0.0)
        make_identity(nc, ident[:])
        make_identity(nc, ident_bf[:])

        def load_we(e):
            nc.sync.dma_start(out=we_raw[e][:], in_=we[e].rearrange("(p j) n -> p (j n)", j=4))

        def load_wg(f):
            nc.sync.dma_start(
                out=wg_w[f][:].bitcast(I32).rearrange("p (s w) -> p s w", s=PASSES),
                in_=wg_words[f].bitcast(I32).rearrange("s p w -> p s w"),
            )

        def load_x(s):
            nc.sync.dma_start(out=x_w[s][:], in_=x_words[s].rearrange("p t d -> p (t d)").bitcast(I32))

        nc.sync.dma_start(offs_t[:], offs)
        load_x(0)
        for q in range(4):
            nc.sync.dma_start(
                out=x_s[32 * q : 32 * q + 4, :].bitcast(I32).rearrange("b (s w) -> b s w", s=PASSES),
                in_=x_scales[:, 4 * q : 4 * q + 4, :].bitcast(I32).rearrange("s b w -> b s w"),
            )
        load_x(1)
        load_we(4)
        load_we(5)
        load_wg(1)
        for q in range(4):
            nc.sync.dma_start(
                out=wg_s[32 * q : 32 * q + 4, :].bitcast(I32).rearrange("b (a w) -> b a w", a=G * PASSES),
                in_=wg_scales[:, :, 4 * q : 4 * q + 4, :].bitcast(I32).rearrange("f s b w -> b (f s) w"),
            )
        nc.sync.dma_start(offs2_t[:], offs2)
        load_we(6)
        load_wg(0)
        for e in (7, 0, 1, 2, 3):
            load_we(e)
        nc.sync.dma_start(dst_t[:], dst)
        nc.sync.dma_start(out=gate_t[1][:], in_=gate[:, C1:])
        nc.sync.dma_start(out=gate_t[0][:], in_=gate[:, :C1])

        def entries(list_tile, c):
            return list_tile[:, c * LIST_COLS : (c + 1) * LIST_COLS]

        tok_w, tok_s, sums, turned, we_bf, we_q, picked, woven, a_q, y_ps, y_sb = {}, {}, {}, {}, {}, {}, {}, {}, {}, {}, {}

        def gather_tokens(c):
            for s in range(PASSES):
                w = held.tile([P, PIECE], U32, name=f"tok_w{c}_{s}", tag=f"words{c % 2}_{s}", align_bytes=64)
                b = held.tile([P, PIECE], U8, name=f"tok_s{c}_{s}", tag=f"bytes{c % 2}_{s}", align_bytes=64)
                nc.vector.tensor_copy(b[:], x_s[:, s * T : (s + 1) * T].indirect(entries(offs_t, c)))
                nc.vector.tensor_copy(w[:], x_w[s][:].bitcast(U32).indirect(entries(offs_t, c)))
                tok_w[c, s] = w
                tok_s[c, s] = b

        def first_products(c):
            f = c // 2
            for half in range(2):
                sums[2 * c + half] = first_psum.tile([P, H], F32, name="acc")
            for s in range(PASSES):
                a = f * PASSES + s
                for half in range(2):
                    cols = slice(half * P, (half + 1) * P)
                    nc.tensor.matmul_mx(
                        out=sums[2 * c + half][:],
                        lhsT=tok_w[c, s][:, cols].bitcast(FP8X4),
                        lhsT_scale=tok_s[c, s][:, cols],
                        rhs=wg_w[f][:, s * 2 * H : (s + 1) * 2 * H].bitcast(FP4X4),
                        rhs_scale=wg_s[:, a * H : (a + 1) * H],
                        start=(s == 0),
                        stop=(s == PASSES - 1),
                    )

        def relu_and_turn_pairs(j):
            c, half = j // 2, j % 2
            a_t = held.tile([P, H], BF16, name=f"a_t{j}", align_bytes=64)
            nc.scalar.activation(
                out=a_t[:].rearrange("m (u p v) -> m u p v", u=2, v=2),
                in_=sums[j][:].rearrange("m (p u v) -> m u p v", u=2, v=2),
                func=RELU,
            )
            if half == 0:
                turned[c] = turn_psum.tile([P, 2 * PIECE], F32, name=f"turned{c % 2}")
            for u in range(2):
                at = u * PIECE + half * P
                nc.tensor.transpose(turned[c][:, at : at + P], a_t[:].bitcast(F32)[:, u * P : (u + 1) * P], ident[:])

        def relu_and_turn_planes(j):
            a_t = held.tile([P, H], BF16, name=f"a_t{j}", align_bytes=64)
            nc.scalar.activation(
                out=a_t[:].rearrange("m (t p) -> m t p", t=4),
                in_=sums[j][:].rearrange("m (p t) -> m t p", t=4),
                func=RELU,
            )
            for t in range(4):
                if j == 0 and t % 2 == 0:
                    turned[t // 2] = turn_psum.tile([P, 2 * C1], BF16, name=f"turned{t // 2}")
                at = (t % 2) * C1 + j * P
                nc.tensor.transpose(turned[t // 2][:, at : at + P], a_t[:, t * P : (t + 1) * P], ident_bf[:])

        def keep_pairs(c):
            by_pair = a_pairs[:, C1:].rearrange("p (u m) -> p u m", u=2)
            nc.scalar.copy(
                out=by_pair[:, :, (c - 2) * PIECE : (c - 1) * PIECE],
                in_=turned[c][:].rearrange("p (u m) -> p u m", u=2),
            )

        def keep_planes():
            for t in range(4):
                nc.scalar.copy(out=a_planes[t][:], in_=turned[t // 2][:, (t % 2) * C1 : (t % 2 + 1) * C1])

        def round_we(e, engine):
            if e % 2 == 0:
                we_bf[e // 2] = held.tile([P, 2 * 4 * N], BF16, name=f"we_bf{e // 2}", align_bytes=64)
            w = we_bf[e // 2][:, (e % 2) * 4 * N : (e % 2 + 1) * 4 * N]
            if engine == "gpsimd":
                nc.gpsimd.tensor_scalar(
                    w.rearrange("p (n j) -> p n j", j=4),
                    we_raw[e][:].rearrange("p (j n) -> p n j", j=4),
                    1.0,
                    0.0,
                    MULT,
                    ADD,
                )
            else:
                copy = nc.scalar.copy if engine == "scalar" else nc.vector.tensor_copy
                copy(
                    out=w.rearrange("p (c i j) -> p c j i", i=4, j=4),
                    in_=we_raw[e][:].rearrange("p (j c i) -> p c j i", i=4, j=4),
                )

        def quantise_we(c):
            tag = {2: "words1_1", 3: "woven2", 0: "woven3", 1: "we_codes1"}[c]
            codes = held.tile([P, 2 * N], U32, name=f"we_codes{c}", tag=tag, align_bytes=64)
            scales = held.tile([P, 2 * N], U8, name=f"we_scales{c}", align_bytes=64)
            nc.vector.quantize_mx(out=codes[:].bitcast(FP8X4), scales=scales[:], in_=we_bf[c][:])
            we_q[c] = (codes, scales)

        def gather_pairs(c):
            g = held.tile([P, 2 * PIECE], U32, name=f"picked{c}", align_bytes=64)
            for u in range(2):
                window = a_pairs[:].bitcast(U32)[:, u * C1 : (u + 2) * C1]
                nc.vector.tensor_copy(g[:, u * PIECE : (u + 1) * PIECE], window.indirect(entries(offs2_t, c)))
            picked[c] = g

        def weave(c):
            w = held.tile([P, 2 * PIECE], U32, name=f"woven{c}", tag=f"woven{c}", align_bytes=64)
            nc.scalar.copy(
                out=w[:].rearrange("p (m u) -> p m u", u=2),
                in_=picked[c][:].rearrange("p (u m) -> p m u", u=2),
            )
            woven[c] = w

        def gather_planes(c):
            g = held.tile([P, 4 * PIECE], BF16, name=f"picked{c}", tag="picked_planes", align_bytes=64)
            for t in range(4):
                nc.scalar.activation(g[:, t * PIECE : (t + 1) * PIECE], a_planes[t][:].indirect(entries(offs2_t, c)), COPY)
            picked[c] = g

        def weave_planes(c):
            w = held.tile([P, 2 * PIECE], U32, name=f"woven{c}", align_bytes=64)
            nc.scalar.copy(
                out=w[:].bitcast(BF16).rearrange("p (m i t) -> p m t i", i=4, t=4),
                in_=picked[c][:].rearrange("p (t m i) -> p m t i", i=4, t=4),
            )
            woven[c] = w

        def quantise_a(c):
            codes = held.tile([P, PIECE], U32, name=f"a_codes{c}", align_bytes=64)
            scales = held.tile([P, PIECE], U8, name=f"a_scales{c}", align_bytes=64)
            nc.vector.quantize_mx(out=codes[:].bitcast(FP8X4), scales=scales[:], in_=woven[c][:].bitcast(BF16))
            a_q[c] = (codes, scales)

        def second_product(c):
            acc = second_psum.tile([P, 2 * PIECE], F32, name="y_acc")
            for h in range(N // P):
                for half in range(2):
                    w_codes, w_scales = we_q[c]
                    a_codes, a_scales = a_q[c]
                    rows = slice(half * N + h * P, half * N + (h + 1) * P)
                    cols = slice(half * C2, (half + 1) * C2)
                    at = h * PIECE + half * C2
                    nc.tensor.matmul_mx(
                        out=acc[:, at : at + C2],
                        lhsT=w_codes[:, rows].bitcast(FP8X4),
                        lhsT_scale=w_scales[:, rows],
                        rhs=a_codes[:, cols].bitcast(FP8X4),
                        rhs_scale=a_scales[:, cols],
                        start=True,
                        stop=True,
                    )
            y_ps[c] = acc

        def keep_y(c, h):
            y = held.tile([P, PIECE], F32, name=f"y{c}_{h}")
            nc.scalar.copy(out=y[:], in_=y_ps[c][:, h * PIECE : (h + 1) * PIECE])
            y_sb[c, h] = y

        def scatter(c, h):
            nc.vector.tensor_tensor(
                result[h][:].indirect(entries(dst_t, c)),
                y_sb[c, h][:],
                gate_t[c // 2][:, (c % 2) * PIECE : (c % 2 + 1) * PIECE],
                MULT,
            )

        def first_level(c):
            gather_tokens(c)
            first_products(c)

        def put_back(c, h):
            keep_y(c, h)
            scatter(c, h)

        def second_level(c):
            quantise_a(c)
            second_product(c)

        first_level(2)
        first_level(3)
        round_we(4, "scalar")
        round_we(5, "scalar")
        for c in (2, 3):
            relu_and_turn_pairs(2 * c)
            relu_and_turn_pairs(2 * c + 1)
            keep_pairs(c)
        first_level(0)
        first_level(1)
        for e in (6, 7, 0, 1):
            round_we(e, "gpsimd")
        gather_pairs(2)
        gather_pairs(3)
        for j in range(4):
            relu_and_turn_planes(j)
        weave(2)
        quantise_we(2)
        second_level(2)
        keep_planes()
        weave(3)
        quantise_we(3)
        second_level(3)
        quantise_we(0)
        round_we(2, "vector")
        put_back(2, 0)
        put_back(2, 1)
        gather_planes(0)
        put_back(3, 0)
        weave_planes(0)
        second_level(0)
        put_back(3, 1)
        gather_planes(1)
        put_back(0, 0)
        weave_planes(1)
        quantise_a(1)
        round_we(3, "scalar")
        quantise_we(1)
        put_back(0, 1)
        second_product(1)
        put_back(1, 0)
        put_back(1, 1)
        for h in range(2):
            nc.sync.dma_start(out=out[h * P : (h + 1) * P, :], in_=result[h][:])
